import numpy as np
import ml_dtypes


def mxq(x, axis, fmt="e4m3"):
    dtype, down = {"e4m3": (ml_dtypes.float8_e4m3fn, 7), "e5m2": (ml_dtypes.float8_e5m2, 14)}[fmt]
    v = np.moveaxis(np.asarray(x, np.float32).astype(ml_dtypes.bfloat16).astype(np.float64), axis, -1)
    blocks = v.reshape(v.shape[:-1] + (-1, 32))
    amax = np.abs(blocks).max(-1, keepdims=True)
    byte = np.maximum(np.where(amax > 0, np.frexp(amax)[1] - 1 + 127, 0) - down, 1)
    scale = np.exp2(byte - 127.0)
    codes = (blocks / scale).astype(np.float32).astype(dtype).astype(np.float64)
    return np.moveaxis((codes * scale).reshape(v.shape), -1, axis)


WIDE = False


def mx_kscale(k):
    if not WIDE:
        return np.ones(k)
    levels = np.array([10, -10, 5, -5, 0])
    if k % 512:
        return np.exp2(np.random.permutation(np.resize(levels, k // 32))).repeat(32)
    a = np.empty((k // 512, 16))
    for p in range(k // 512):
        a[p, :8] = np.random.permutation(np.resize(levels, 8))
        for g in range(8):
            far = levels[np.abs(levels - a[p, g]) >= 10]
            a[p, g + 8] = far[np.random.randint(len(far))]
    return np.exp2(a.ravel()).repeat(32)


def f64(x):
    return np.asarray(x).astype(np.float64)


def striped(idx):
    return np.tile(idx.reshape(-1, 16).T, (8, 1)).astype(np.uint16)


def unstriped(offs):
    return offs[:16].T.reshape(-1).astype(np.int64)


E2M1 = np.array([0.0, 0.5, 1.0, 1.5, 2.0, 3.0, 4.0, 6.0, -0.0, -0.5, -1.0, -1.5, -2.0, -3.0, -4.0, -6.0])


def pack_weight(w, fmt):
    k, n = w.shape
    w = f64(np.asarray(w, np.float32).astype(ml_dtypes.bfloat16)).reshape(k // 32, 32, n)
    amax = np.abs(w).max(1)
    if fmt == "e4m3":
        byte = np.frexp(amax)[1] - 1 + 127 - 7
    else:
        mant, ex = np.frexp(amax / 6.0)
        byte = np.where(mant > 0.5, ex, ex - 1) + 127
    byte = np.clip(np.where(amax > 0, byte, 1), 1, 254)
    scaled = (w * np.exp2(127.0 - byte)[:, None, :]).reshape(k, n).astype(np.float32)
    by_word = np.ascontiguousarray(scaled.reshape(k // 512, 128, 4, n).transpose(0, 1, 3, 2))
    if fmt == "e4m3":
        words = by_word.astype(ml_dtypes.float8_e4m3fn).view(np.uint8)
    else:
        c = by_word.astype(ml_dtypes.float4_e2m1fn).view(np.uint8) & 0xF
        words = (c[..., 0::2] | (c[..., 1::2] << 4)).reshape(k // 512, 128, 2 * n)
    return np.ascontiguousarray(words), np.ascontiguousarray(byte.astype(np.uint8).reshape(k // 512, 16, n))


def unpack_weight(words, scales, fmt):
    g, _, n = scales.shape
    words = np.ascontiguousarray(words).reshape(g, 128, n, -1)
    if fmt == "e4m3":
        vals = words.view(ml_dtypes.float8_e4m3fn).astype(np.float64)
    else:
        nib = np.empty((g, 128, n, 4), np.uint8)
        nib[..., 0::2] = words & 0xF
        nib[..., 1::2] = words >> 4
        vals = E2M1[nib]
    vals = vals * np.repeat(np.exp2(scales.astype(np.float64) - 127.0), 8, axis=1)[..., None]
    return vals.transpose(0, 1, 3, 2).reshape(g * 512, n)


def gelu(v):
    return 0.5 * v * (1.0 + np.tanh(np.sqrt(2.0 / np.pi) * (v + 0.044715 * v**3)))


def striped8(idx):
    return np.concatenate([v.reshape(-1, 16).T for v in idx]).astype(np.uint16)


def unstriped8(offs):
    return np.stack([offs[16 * g:16 * g + 16].T.reshape(-1) for g in range(8)]).astype(np.int64)


def heads(h, wgt, idx8):
    r = np.arange(h.shape[0])
    return wgt[r // 4 % 128] * h[r[:, None], idx8[r % 512 // 64]]


def put_heads(h, wgs, idx8, t2):
    r = np.arange(h.shape[0])
    page = np.zeros((h.shape[0], t2))
    page[r[:, None], idx8[r % 512 // 64]] = wgs[r // 4 % 128] * h
    return page


K, H, N, T, S, P, T2 = 512, 1024, 384, 4096, 1024, 1024, 2048


def setup_inputs():
    n = np.random.standard_normal
    s = mx_kscale(K)[:, None]
    u = mx_kscale(H)[:, None]
    d = {}
    d["tab_words"], d["tab_scales"] = pack_weight(n((K, T)) * s, "e4m3")
    d["offs"] = striped(np.random.permutation(T)[:S])
    d["offs2"] = striped8(np.stack([np.random.permutation(T2)[:S] for _ in range(8)]))
    d["offs3"] = striped8(np.stack([np.random.permutation(T2)[:P] for _ in range(8)]))
    d["w1"] = (1.5 * n((K, H)) / s / K**0.5).astype(np.float32)
    d["gain"] = (1.5 * np.exp(0.3 * n(H)) * u[:, 0]).astype(np.float32)
    d["wgs"] = np.repeat(np.random.uniform(0.5, 2.0, (8, S)), 16, axis=0).astype(np.float32)
    d["wgt"] = np.repeat(np.random.uniform(0.5, 2.0, (8, P)), 16, axis=0).astype(np.float32)
    d["foam"] = (n((H, P)) * u).astype(np.float32)
    d["w4_words"], d["w4_scales"] = pack_weight(n((H, N)) / u / H**0.5, "e2m1")
    d["w5"] = (n((H, N)) / u / H**0.5).astype(np.float32)
    return d


def reference(tab_words, tab_scales, offs, offs2, offs3, w1, gain, wgs, wgt, foam, w4_words, w4_scales, w5):
    v = unpack_weight(tab_words, tab_scales, "e4m3")[:, unstriped(offs)]
    load = mxq(f64(w1), 0, "e4m3").T @ v
    h = f64(gain)[:, None] * (1.0 / (1.0 + np.abs(load)))
    page = put_heads(h, f64(wgs), unstriped8(offs2), T2)
    x = heads(page, f64(wgt), unstriped8(offs3))
    z = mxq(x + f64(foam), 0, "e4m3")
    w4 = unpack_weight(w4_words, w4_scales, "e2m1")
    wear = w4.T @ z
    rest = mxq(f64(w5), 0, "e4m3").T @ z
    return np.abs(wear) - rest

@@ -1,0 +1,338 @@
+from contextlib import ExitStack
+
+import concourse.mybir as mybir
+from concourse.masks import make_identity
+
+K, H, N, T, S, M, T2 = 512, 1024, 384, 4096, 1024, 1024, 2048
+FLOPS = 2 * K * H * S + 2 * 2 * H * N * M
+
+F32 = mybir.dt.float32
+BF16 = mybir.dt.bfloat16
+I32 = mybir.dt.int32
+U32 = mybir.dt.uint32
+U16 = mybir.dt.uint16
+U8 = mybir.dt.uint8
+FP8X4 = mybir.dt.float8_e4m3fn_x4
+FP4X4 = mybir.dt.float4_e2m1fn_x4
+ALU = mybir.AluOpType
+ACT = mybir.ActivationFunctionType
+
+P = 128
+PAGES = 3
+H_RING = 3
+X_RING = 4
+PIECES = (256, 256, 256, 256)
+
+
+def tile_list_spring_fatigue_features_kernel(
+    tc, tab_words, tab_scales, offs, offs2, offs3, w1, gain, wgs, wgt, foam, w4_words, w4_scales, w5, out
+):
+    nc = tc.nc
+    with ExitStack() as ctx:
+        lists = ctx.enter_context(tc.tile_pool(name="lists", bufs=1))
+        keep = ctx.enter_context(tc.tile_pool(name="keep", bufs=1))
+        ring = ctx.enter_context(tc.tile_pool(name="ring", bufs=3))
+        psum = ctx.enter_context(tc.psum_pool(name="psum", bufs=1))
+
+        def bank(k):
+            return psum.tile([P, 512], F32, name=f"bank{k}", tag=f"bank{k}")
+
+        offs_t = lists.tile([P, S // 16], U16, name="offs_t")
+        offs2_t = lists.tile([P, S // 16], U16, name="offs2_t")
+        offs3_t = lists.tile([P, M // 16], U16, name="offs3_t")
+
+        tab_s = keep.tile([P, T], U8, name="tab_s", align_bytes=64)
+        w4_s = keep.tile([P, 2 * N], U8, name="w4_s", align_bytes=64)
+        pages = [keep.tile([P, T2], F32, name=f"page{k}", align_bytes=64) for k in range(PAGES)]
+        nc.vector.memset(tab_s[:].bitcast(I32), 0)
+        nc.vector.memset(w4_s[:].bitcast(I32), 0)
+        for page in pages:
+            nc.vector.memset(page[:], 0.0)
+        ident = keep.tile([P, P], F32, name="ident", align_bytes=64)
+        make_identity(nc, ident[:])
+
+        tab_w = keep.tile([P, T], U32, name="tab_w", align_bytes=64)
+        w1_raw = [keep.tile([P, 4, 512], F32, name=f"w1_raw{b}") for b in range(2)]
+        gain_t = keep.tile([P, 2, 4], F32, name="gain_t")
+        wgs_t = [keep.tile([P, 512], F32, name=f"wgs{half}") for half in range(2)]
+        wgt_t = keep.tile([P, M], F32, name="wgt_t")
+        foam_t = [keep.tile([P, 2, M], F32, name=f"foam{pair}", align_bytes=64) for pair in range(4)]
+        w5_raw = keep.tile([P, 2, 4, N], F32, name="w5_raw")
+        w4_w = keep.tile([P, 2 * 2 * N], U8, name="w4_w", align_bytes=64)
+
+        w1_rows = w1.rearrange("(p j) c -> p j c", j=4)
+        foam_rows = foam.rearrange("(b p u e) m -> b u p e m", b=2, u=2, e=2)
+        nc.sync.dma_start(offs_t[:], offs)
+        nc.sync.dma_start(w1_raw[0][:], w1_rows[:, :, 0:512])
+        for q in range(4):
+            nc.sync.dma_start(
+                tab_s[32 * q : 32 * q + 4, :].bitcast(I32), tab_scales[0, 4 * q : 4 * q + 4, :].bitcast(I32)
+            )
+        nc.sync.dma_start(tab_w[:].bitcast(I32), tab_words[0].rearrange("p t i -> p (t i)").bitcast(I32))
+        nc.sync.dma_start(gain_t[:], gain.rearrange("(b p t) -> p b t", b=2, t=4))
+        nc.sync.dma_start(wgs_t[0][:], wgs[:, 0:512])
+        nc.sync.dma_start(offs2_t[:], offs2)
+        nc.sync.dma_start(wgs_t[1][:], wgs[:, 512:1024])
+        nc.sync.dma_start(w1_raw[1][:], w1_rows[:, :, 512:1024])
+        nc.sync.dma_start(offs3_t[:], offs3)
+        nc.sync.dma_start(wgt_t[:], wgt)
+        for pair in range(2):
+            nc.sync.dma_start(foam_t[pair][:], foam_rows[0, pair])
+        for b in range(2):
+            nc.sync.dma_start(w5_raw[:, b], w5[512 * b : 512 * (b + 1), :].rearrange("(p j) n -> p j n", j=4))
+        nc.sync.dma_start(
+            w4_w[:].bitcast(I32).rearrange("p (b c) -> p b c", b=2), w4_words.bitcast(I32).rearrange("b p c -> p b c")
+        )
+        for q in range(4):
+            nc.sync.dma_start(
+                w4_s[32 * q : 32 * q + 4, :].bitcast(I32).rearrange("r (b c) -> r b c", b=2),
+                w4_scales[:, 4 * q : 4 * q + 4, :].bitcast(I32).rearrange("b r c -> r b c"),
+            )
+        for pair in range(2):
+            nc.sync.dma_start(foam_t[2 + pair][:], foam_rows[1, pair])
+
+        w1_bf = keep.tile([P, 2048], BF16, name="w1_bf", align_bytes=64)
+        w1_c = [keep.tile([P, 512], U32, name=f"w1_c{b}", align_bytes=64) for b in range(2)]
+        w1_s = [keep.tile([P, 512], U8, name=f"w1_s{b}", align_bytes=64) for b in range(2)]
+
+        def w1_views(b):
+            return (
+                w1_bf[:].rearrange("p (t m j) -> p m t j", t=4, j=4),
+                w1_raw[b][:].rearrange("p j (m t) -> p m t j", t=4),
+            )
+
+        def quantise_w1(b):
+            nc.vector.quantize_mx(out=w1_c[b][:].bitcast(FP8X4), scales=w1_s[b][:], in_=w1_bf[:])
+
+        v_s = keep.tile([P, S], U8, name="v_s", align_bytes=64)
+        v_w = [keep.tile([P, 512], U32, name=f"v_w{half}", align_bytes=64) for half in range(2)]
+        nc.vector.tensor_copy(v_s[:], tab_s[:].indirect(offs_t[:]))
+        nc.vector.tensor_copy(*w1_views(0))
+        quantise_w1(0)
+        for half in range(2):
+            nc.vector.tensor_copy(v_w[half][:], tab_w[:].indirect(offs_t[:, 32 * half : 32 * (half + 1)]))
+
+        work = keep.tile([P, X_RING, S], F32, name="work", align_bytes=64)
+        h_t = [keep.tile([P, S], F32, name=f"h{k}") for k in range(H_RING)]
+        gw_t = [keep.tile([P, S], F32, name=f"gw{k}") for k in range(H_RING)]
+
+        def features(i, spans):
+            b, t = divmod(i, 4)
+            a = work[:, (i - 1) % X_RING, :]
+            for lo, hi in spans:
+                for half in range(lo // 512, hi // 512):
+                    cols = slice(512 * half, 512 * (half + 1))
+                    nc.scalar.activation(
+                        gw_t[i % H_RING][:, cols], wgs_t[half][:], ACT.Copy, scale=gain_t[:, b, t : t + 1]
+                    )
+                    load = bank(half)
+                    nc.tensor.matmul_mx(
+                        out=load[:],
+                        lhsT=w1_c[b][:, P * t : P * (t + 1)].bitcast(FP8X4),
+                        lhsT_scale=w1_s[b][:, P * t : P * (t + 1)],
+                        rhs=v_w[half][:].bitcast(FP8X4),
+                        rhs_scale=v_s[:, cols],
+                        start=True,
+                        stop=True,
+                    )
+                    nc.scalar.activation(a[:, cols], load[:], ACT.Abs)
+                nc.scalar.activation(a[:, lo:hi], a[:, lo:hi], ACT.Square, bias=1.0)
+                nc.scalar.activation(h_t[i % H_RING][:, lo:hi], a[:, lo:hi], ACT.Abs_reciprocal_sqrt)
+
+        def scatter(i, spans):
+            for lo, hi in spans:
+                nc.vector.tensor_tensor(
+                    pages[i % PAGES][:].indirect(offs2_t[:, lo // 16 : hi // 16]),
+                    h_t[i % H_RING][:, lo:hi],
+                    gw_t[i % H_RING][:, lo:hi],
+                    ALU.mult,
+                )
+
+        def gather(i, lo, hi):
+            nc.vector.tensor_tensor(
+                work[:, i % X_RING, lo:hi],
+                pages[i % PAGES][:].indirect(offs3_t[:, lo // 16 : hi // 16]),
+                wgt_t[:, lo:hi],
+                ALU.mult,
+            )
+
+        z_turned = [
+            [keep.tile([P, 512], BF16, name=f"z_turned{u}_{k}", align_bytes=64) for k in range(4)] for u in range(2)
+        ]
+
+        def add_foam(pair):
+            u = pair % 2
+            for k in range(4):
+                acc = bank(2 + k)
+                sources = [foam_t[pair][:, e, :] for e in range(2)]
+                sources = sources + [work[:, (2 * pair + e) % X_RING, :] for e in range(2)]
+                steps = [(s, c) for s in range(4) for c in range(2)]
+                for n, (s, c) in enumerate(steps):
+                    col = 256 * c + P * (s % 2)
+                    m0 = 256 * k + P * c
+                    nc.tensor.matmul(
+                        acc[:, col : col + P],
+                        sources[s][:, m0 : m0 + P],
+                        ident[:],
+                        start=(n == 0),
+                        stop=(n == len(steps) - 1),
+                        is_transpose=True,
+                    )
+                nc.scalar.copy(
+                    z_turned[u][k][:].rearrange("m (c p e) -> m c p e", c=2, e=2),
+                    acc[:].rearrange("m (c e p) -> m c p e", c=2, e=2),
+                )
+
+        z_bf0 = keep.tile([P, 4 * M], BF16, name="z_bf0", align_bytes=64)
+        z_c0 = keep.tile([P, M], U32, name="z_c0", align_bytes=64)
+        z_s0 = keep.tile([P, M], U8, name="z_s0", align_bytes=64)
+
+        def turn_back_first():
+            for k in range(4):
+                acc = bank(6 + k % 2)
+                for u in range(2):
+                    for c in range(2):
+                        col = 256 * u + P * c
+                        nc.tensor.transpose(
+                            acc[:, col : col + P], z_turned[u][k][:].bitcast(F32)[:, P * c : P * (c + 1)], ident[:]
+                        )
+                nc.scalar.copy(
+                    z_bf0[:].bitcast(F32)[:, 512 * k : 512 * (k + 1)].rearrange("p (m u) -> p m u", u=2),
+                    acc[:].rearrange("p (u m) -> p m u", u=2),
+                )
+
+        starts = [sum(PIECES[:n]) for n in range(len(PIECES))]
+        z_pairs = [
+            keep.tile([P, 4 * w], BF16, name=f"z_pairs{n}", align_bytes=64) for n, w in enumerate(PIECES)
+        ]
+
+        def turn_back_second():
+            for k2 in range(2):
+                acc = bank(6 + k2)
+                for c in range(4):
+                    k, cc = divmod(4 * k2 + c, 2)
+                    nc.tensor.transpose(
+                        acc[:, P * c : P * (c + 1)], z_turned[0][k][:].bitcast(F32)[:, P * cc : P * (cc + 1)], ident[:]
+                    )
+                for n, w in enumerate(PIECES):
+                    if starts[n] // 512 == k2:
+                        lo = starts[n] - 512 * k2
+                        nc.scalar.copy(z_pairs[n][:].bitcast(F32)[:, 0:w], acc[:, lo : lo + w])
+
+        w5_bf = keep.tile([P, 2 * 4 * N], BF16, name="w5_bf", align_bytes=64)
+        w5_c = keep.tile([P, 2 * N], U32, name="w5_c", align_bytes=64)
+        w5_s = keep.tile([P, 2 * N], U8, name="w5_s", align_bytes=64)
+
+        def prepare_w5():
+            for b in range(2):
+                nc.scalar.copy(
+                    w5_bf[:, 4 * N * b : 4 * N * (b + 1)].rearrange("p (n j) -> p n j", j=4),
+                    w5_raw[:, b].rearrange("p j n -> p n j"),
+                )
+            for lo, hi in ((0, 512), (512, 768)):
+                nc.vector.quantize_mx(
+                    out=w5_c[:, lo:hi].bitcast(FP8X4), scales=w5_s[:, lo:hi], in_=w5_bf[:, 4 * lo : 4 * hi]
+                )
+
+        whole = [(0, S)]
+        halves = [(0, 512), (512, S)]
+        features(0, halves)
+        scatter(0, halves)
+        features(1, whole)
+        nc.scalar.copy(*w1_views(1))
+        quantise_w1(1)
+        for i in range(7):
+            scatter(i + 1, whole)
+            gather(i, 0, M)
+            if i + 2 < 8:
+                features(i + 2, whole)
+            if i == 1:
+                prepare_w5()
+            if i in (2, 4, 6):
+                add_foam(i // 2 - 1)
+            if i == 4:
+                turn_back_first()
+                nc.vector.quantize_mx(out=z_c0[:].bitcast(FP8X4), scales=z_s0[:], in_=z_bf0[:])
+        turn_back_second()
+
+        def passes(sums, b, codes, scales):
+            for nt in range(3):
+                col = N * b + P * nt
+                flags = dict(start=(b == 0 and nt == 0), stop=(b == 1 and nt == 2))
+                nc.tensor.matmul_mx(
+                    out=sums[0][:, P * nt : P * (nt + 1)],
+                    lhsT=w4_w[:, 2 * col : 2 * (col + P)].bitcast(FP4X4),
+                    lhsT_scale=w4_s[:, col : col + P],
+                    rhs=codes.bitcast(FP8X4),
+                    rhs_scale=scales,
+                    **flags,
+                )
+                nc.tensor.matmul_mx(
+                    out=sums[1][:, P * nt : P * (nt + 1)],
+                    lhsT=w5_c[:, col : col + P].bitcast(FP8X4),
+                    lhsT_scale=w5_s[:, col : col + P],
+                    rhs=codes.bitcast(FP8X4),
+                    rhs_scale=scales,
+                    **flags,
+                )
+
+        def open_sums(chunk):
+            sums = (bank(2 * chunk % 8), bank((2 * chunk + 1) % 8))
+            cols = slice(P * chunk, P * (chunk + 1))
+            passes(sums, 0, z_c0[:, cols], z_s0[:, cols])
+            return sums
+
+        opened = {chunk: open_sums(chunk) for chunk in range(4)}
+        out_rows = out.rearrange("(nt p) m -> p nt m", p=P)
+        quantised = {}
+
+        def make_z(n):
+            lo, w = starts[n], PIECES[n]
+            gather(7, lo, lo + w)
+            nc.vector.tensor_tensor(
+                z_pairs[n][:, 2 * w : 4 * w].rearrange("p (c i e) -> p c e i", i=4, e=2),
+                work[:, 2:4, lo : lo + w].rearrange("p e (c i) -> p c e i", i=4),
+                foam_t[3][:, :, lo : lo + w].rearrange("p e (c i) -> p c e i", i=4),
+                ALU.add,
+            )
+            z_bf = z_bf0[:, 4 * lo : 4 * (lo + w)]
+            nc.scalar.copy(
+                z_bf0[:].bitcast(F32)[:, 2 * lo : 2 * (lo + w)].rearrange("p (m u) -> p m u", u=2),
+                z_pairs[n][:].bitcast(F32).rearrange("p (u m) -> p m u", u=2),
+            )
+            quantised[n] = z_bf
+
+        def quantise_z(n):
+            w = PIECES[n]
+            z_c = keep.tile([P, w], U32, name=f"z_c1_{n}", align_bytes=64)
+            z_s = keep.tile([P, w], U8, name=f"z_s1_{n}", align_bytes=64)
+            nc.vector.quantize_mx(out=z_c[:].bitcast(FP8X4), scales=z_s[:], in_=quantised[n])
+            quantised[n] = (z_c, z_s)
+
+        def finish(n):
+            lo, w = starts[n], PIECES[n]
+            z_c, z_s = quantised[n]
+            result = keep.tile([P, 3, w], F32, name=f"result{n}")
+            for c in range(w // P):
+                chunk = lo // P + c
+                sums = opened[chunk] if chunk in opened else open_sums(chunk)
+                cols = slice(P * c, P * (c + 1))
+                passes(sums, 1, z_c[:, cols], z_s[:, cols])
+                wear = ring.tile([P, N], F32, name="wear")
+                nc.scalar.activation(wear[:], sums[0][:, 0:N], ACT.Abs)
+                nc.vector.tensor_tensor(
+                    result[:, :, cols],
+                    wear[:].rearrange("p (nt m) -> p nt m", nt=3),
+                    sums[1][:, 0:N].rearrange("p (nt m) -> p nt m", nt=3),
+                    ALU.subtract,
+                )
+            nc.sync.dma_start(out_rows[:, :, lo : lo + w], result[:])
+
+        count = len(PIECES)
+        for step in range(count + 2):
+            if step < count:
+                make_z(step)
+            if 1 <= step <= count:
+                quantise_z(step - 1)
+            if step >= 2:
+                finish(step - 2)

@@ -21,7 +21,7 @@ P = 128
 PAGES = 3
 H_RING = 3
 X_RING = 4
-PIECES = (256, 256, 256, 256)
+PIECES = (256, 256, 256, 128, 128)
 
 
 def tile_list_spring_fatigue_features_kernel(
@@ -31,6 +31,7 @@ def tile_list_spring_fatigue_features_kernel(
     with ExitStack() as ctx:
         lists = ctx.enter_context(tc.tile_pool(name="lists", bufs=1))
         keep = ctx.enter_context(tc.tile_pool(name="keep", bufs=1))
+        early = ctx.enter_context(tc.tile_pool(name="early", bufs=1))
         ring = ctx.enter_context(tc.tile_pool(name="ring", bufs=3))
         psum = ctx.enter_context(tc.psum_pool(name="psum", bufs=1))
 
@@ -41,110 +42,108 @@ def tile_list_spring_fatigue_features_kernel(
         offs2_t = lists.tile([P, S // 16], U16, name="offs2_t")
         offs3_t = lists.tile([P, M // 16], U16, name="offs3_t")
 
-        tab_s = keep.tile([P, T], U8, name="tab_s", align_bytes=64)
-        w4_s = keep.tile([P, 2 * N], U8, name="w4_s", align_bytes=64)
-        pages = [keep.tile([P, T2], F32, name=f"page{k}", align_bytes=64) for k in range(PAGES)]
-        nc.vector.memset(tab_s[:].bitcast(I32), 0)
-        nc.vector.memset(w4_s[:].bitcast(I32), 0)
-        for page in pages:
-            nc.vector.memset(page[:], 0.0)
+        tab_s = keep.tile([P, T // 4], I32, name="tab_s", tag="slot_d", align_bytes=64)
+        pages = [keep.tile([P, T2], F32, name="page0", align_bytes=64)]
+        nc.vector.memset(tab_s[:], 0)
+        ident_made = early.tile([P, P], F32, name="ident_made", align_bytes=64, offset=4 * T - 256)
         ident = keep.tile([P, P], F32, name="ident", align_bytes=64)
-        make_identity(nc, ident[:])
-
-        tab_w = keep.tile([P, T], U32, name="tab_w", align_bytes=64)
-        w1_raw = [keep.tile([P, 4, 512], F32, name=f"w1_raw{b}") for b in range(2)]
-        gain_t = keep.tile([P, 2, 4], F32, name="gain_t")
-        wgs_t = [keep.tile([P, 512], F32, name=f"wgs{half}") for half in range(2)]
-        wgt_t = keep.tile([P, M], F32, name="wgt_t")
-        foam_t = [keep.tile([P, 2, M], F32, name=f"foam{pair}", align_bytes=64) for pair in range(4)]
-        w5_raw = keep.tile([P, 2, 4, N], F32, name="w5_raw")
-        w4_w = keep.tile([P, 2 * 2 * N], U8, name="w4_w", align_bytes=64)
+        make_identity(nc, ident_made[:])
+        nc.gpsimd.tensor_copy(ident[:], ident_made[:])
+        for page in pages:
+            nc.vector.memset(page[:].bitcast(I32), 0)
+        warm = keep.tile([P, 1], F32, name="warm")
+        nc.scalar.activation(warm[:], ident[:, 0:1], ACT.Abs_reciprocal_sqrt, bias=1.0)
 
         w1_rows = w1.rearrange("(p j) c -> p j c", j=4)
         foam_rows = foam.rearrange("(b p u e) m -> b u p e m", b=2, u=2, e=2)
+        gain_t = keep.tile([P, 2, 4], F32, name="gain_t")
+        w1_raw0 = keep.tile([P, 4, 512], F32, name="w1_raw0", tag="slot_a", align_bytes=64)
+        tab_w = early.tile([P, T], U32, name="tab_w", align_bytes=64, offset=0)
         nc.sync.dma_start(offs_t[:], offs)
-        nc.sync.dma_start(w1_raw[0][:], w1_rows[:, :, 0:512])
+        nc.sync.dma_start(w1_raw0[:], w1_rows[:, :, 0:512])
         for q in range(4):
             nc.sync.dma_start(
-                tab_s[32 * q : 32 * q + 4, :].bitcast(I32), tab_scales[0, 4 * q : 4 * q + 4, :].bitcast(I32)
+                tab_s[32 * q : 32 * q + 4, :], tab_scales[0, 4 * q : 4 * q + 4, :].bitcast(I32)
             )
         nc.sync.dma_start(tab_w[:].bitcast(I32), tab_words[0].rearrange("p t i -> p (t i)").bitcast(I32))
+        wgs_t = early.tile([P, S], F32, name="wgs_t", align_bytes=64, offset=4 * T)
+        nc.sync.dma_start(wgs_t[:], wgs)
         nc.sync.dma_start(gain_t[:], gain.rearrange("(b p t) -> p b t", b=2, t=4))
-        nc.sync.dma_start(wgs_t[0][:], wgs[:, 0:512])
         nc.sync.dma_start(offs2_t[:], offs2)
-        nc.sync.dma_start(wgs_t[1][:], wgs[:, 512:1024])
-        nc.sync.dma_start(w1_raw[1][:], w1_rows[:, :, 512:1024])
         nc.sync.dma_start(offs3_t[:], offs3)
-        nc.sync.dma_start(wgt_t[:], wgt)
-        for pair in range(2):
-            nc.sync.dma_start(foam_t[pair][:], foam_rows[0, pair])
-        for b in range(2):
-            nc.sync.dma_start(w5_raw[:, b], w5[512 * b : 512 * (b + 1), :].rearrange("(p j) n -> p j n", j=4))
-        nc.sync.dma_start(
-            w4_w[:].bitcast(I32).rearrange("p (b c) -> p b c", b=2), w4_words.bitcast(I32).rearrange("b p c -> p b c")
-        )
-        for q in range(4):
-            nc.sync.dma_start(
-                w4_s[32 * q : 32 * q + 4, :].bitcast(I32).rearrange("r (b c) -> r b c", b=2),
-                w4_scales[:, 4 * q : 4 * q + 4, :].bitcast(I32).rearrange("b r c -> r b c"),
-            )
-        for pair in range(2):
-            nc.sync.dma_start(foam_t[2 + pair][:], foam_rows[1, pair])
 
-        w1_bf = keep.tile([P, 2048], BF16, name="w1_bf", align_bytes=64)
+        def load_foam(pair):
+            tile = keep.tile([P, 2, M], F32, name=f"foam{pair}", tag=("slot_b", "slot_e")[pair % 2], align_bytes=64)
+            nc.sync.dma_start(tile[:], foam_rows[pair // 2, pair % 2])
+            return tile
+
         w1_c = [keep.tile([P, 512], U32, name=f"w1_c{b}", align_bytes=64) for b in range(2)]
         w1_s = [keep.tile([P, 512], U8, name=f"w1_s{b}", align_bytes=64) for b in range(2)]
 
-        def w1_views(b):
-            return (
-                w1_bf[:].rearrange("p (t m j) -> p m t j", t=4, j=4),
-                w1_raw[b][:].rearrange("p j (m t) -> p m t j", t=4),
+        def prepare_w1(b, raw, copy, tag):
+            rounded = keep.tile([P, 2048], BF16, name=f"w1_bf{b}", tag=tag, align_bytes=64)
+            copy(
+                rounded[:].rearrange("p (t m j) -> p m t j", t=4, j=4),
+                raw[:].rearrange("p j (m t) -> p m t j", t=4),
             )
-
-        def quantise_w1(b):
-            nc.vector.quantize_mx(out=w1_c[b][:].bitcast(FP8X4), scales=w1_s[b][:], in_=w1_bf[:])
+            nc.vector.quantize_mx(out=w1_c[b][:].bitcast(FP8X4), scales=w1_s[b][:], in_=rounded[:])
 
         v_s = keep.tile([P, S], U8, name="v_s", align_bytes=64)
         v_w = [keep.tile([P, 512], U32, name=f"v_w{half}", align_bytes=64) for half in range(2)]
-        nc.vector.tensor_copy(v_s[:], tab_s[:].indirect(offs_t[:]))
-        nc.vector.tensor_copy(*w1_views(0))
-        quantise_w1(0)
+        nc.vector.tensor_copy(v_s[:], tab_s[:].bitcast(U8).indirect(offs_t[:]))
+        prepare_w1(0, w1_raw0, nc.scalar.copy, "slot_b")
         for half in range(2):
             nc.vector.tensor_copy(v_w[half][:], tab_w[:].indirect(offs_t[:, 32 * half : 32 * (half + 1)]))
+
+        w1_raw1 = keep.tile([P, 4, 512], F32, name="w1_raw1", tag="slot_b", align_bytes=64)
+        wgt_t = keep.tile([P, M], F32, name="wgt_t", tag="slot_d", align_bytes=64)
+        for k in range(1, PAGES):
+            page = early.tile([P, T2], F32, name=f"page{k}", align_bytes=64, offset=4 * T2 * (k - 1))
+            nc.gpsimd.memset(page[:], 0.0)
+            pages.append(page)
+        nc.sync.dma_start(w1_raw1[:], w1_rows[:, :, 512:1024])
+        nc.sync.dma_start(wgt_t[:], wgt)
 
         work = keep.tile([P, X_RING, S], F32, name="work", align_bytes=64)
         h_t = [keep.tile([P, S], F32, name=f"h{k}") for k in range(H_RING)]
         gw_t = [keep.tile([P, S], F32, name=f"gw{k}") for k in range(H_RING)]
 
+        first_gw = keep.tile([P, 256], F32, name="first_gw")
+
         def features(i, spans):
             b, t = divmod(i, 4)
             a = work[:, (i - 1) % X_RING, :]
-            for lo, hi in spans:
-                for half in range(lo // 512, hi // 512):
-                    cols = slice(512 * half, 512 * (half + 1))
-                    nc.scalar.activation(
-                        gw_t[i % H_RING][:, cols], wgs_t[half][:], ACT.Copy, scale=gain_t[:, b, t : t + 1]
-                    )
-                    load = bank(half)
+            gw = gw_t[i % H_RING]
+            factor = gain_t[:, b, t : t + 1]
+            for n, (lo, hi) in enumerate(spans):
+                ahead = (i, n) == (0, 0)
+                if ahead:
+                    nc.scalar.activation(first_gw[:], wgs_t[:, lo:hi], ACT.Copy, scale=factor)
+                for c0 in range(lo, hi, 512):
+                    c1 = min(hi, c0 + 512)
+                    half, v0 = divmod(c0, 512)
+                    load = bank(n if i == 0 else half)
                     nc.tensor.matmul_mx(
-                        out=load[:],
+                        out=load[:, 0 : c1 - c0],
                         lhsT=w1_c[b][:, P * t : P * (t + 1)].bitcast(FP8X4),
                         lhsT_scale=w1_s[b][:, P * t : P * (t + 1)],
-                        rhs=v_w[half][:].bitcast(FP8X4),
-                        rhs_scale=v_s[:, cols],
+                        rhs=v_w[half][:, v0 : v0 + c1 - c0].bitcast(FP8X4),
+                        rhs_scale=v_s[:, c0:c1],
                         start=True,
                         stop=True,
                     )
-                    nc.scalar.activation(a[:, cols], load[:], ACT.Abs)
-                nc.scalar.activation(a[:, lo:hi], a[:, lo:hi], ACT.Square, bias=1.0)
+                    nc.scalar.activation(gw[:, c0:c1], load[:, 0 : c1 - c0], ACT.Abs)
+                nc.scalar.activation(a[:, lo:hi], gw[:, lo:hi], ACT.Square, bias=1.0)
                 nc.scalar.activation(h_t[i % H_RING][:, lo:hi], a[:, lo:hi], ACT.Abs_reciprocal_sqrt)
+                if not ahead:
+                    nc.scalar.activation(gw[:, lo:hi], wgs_t[:, lo:hi], ACT.Copy, scale=factor)
 
         def scatter(i, spans):
-            for lo, hi in spans:
+            for n, (lo, hi) in enumerate(spans):
                 nc.vector.tensor_tensor(
                     pages[i % PAGES][:].indirect(offs2_t[:, lo // 16 : hi // 16]),
                     h_t[i % H_RING][:, lo:hi],
-                    gw_t[i % H_RING][:, lo:hi],
+                    first_gw[:] if (i, n) == (0, 0) else gw_t[i % H_RING][:, lo:hi],
                     ALU.mult,
                 )
 
@@ -219,7 +218,7 @@ def tile_list_spring_fatigue_features_kernel(
                         lo = starts[n] - 512 * k2
                         nc.scalar.copy(z_pairs[n][:].bitcast(F32)[:, 0:w], acc[:, lo : lo + w])
 
-        w5_bf = keep.tile([P, 2 * 4 * N], BF16, name="w5_bf", align_bytes=64)
+        w5_bf = keep.tile([P, 2 * 4 * N], BF16, name="w5_bf", tag="slot_f", align_bytes=64)
         w5_c = keep.tile([P, 2 * N], U32, name="w5_c", align_bytes=64)
         w5_s = keep.tile([P, 2 * N], U8, name="w5_s", align_bytes=64)
 
@@ -235,12 +234,14 @@ def tile_list_spring_fatigue_features_kernel(
                 )
 
         whole = [(0, S)]
-        halves = [(0, 512), (512, S)]
+        halves = [(0, 256), (256, 512), (512, S)]
         features(0, halves)
         scatter(0, halves)
         features(1, whole)
-        nc.scalar.copy(*w1_views(1))
-        quantise_w1(1)
+        prepare_w1(1, w1_raw1, nc.scalar.copy, "slot_e")
+        foam_t = {0: load_foam(0)}
+        w5_raw = keep.tile([P, 2, 4, N], F32, name="w5_raw", tag="slot_e", align_bytes=64)
+        nc.sync.dma_start(w5_raw[:], w5.rearrange("(b p j) n -> p b j n", b=2, j=4))
         for i in range(7):
             scatter(i + 1, whole)
             gather(i, 0, M)
@@ -248,12 +249,26 @@ def tile_list_spring_fatigue_features_kernel(
                 features(i + 2, whole)
             if i == 1:
                 prepare_w5()
+                foam_t[1] = load_foam(1)
+                w4_s = keep.tile([P, 2 * N], U8, name="w4_s", tag="slot_f", align_bytes=64)
+                nc.vector.memset(w4_s[:].bitcast(I32), 0)
+                for q in range(4):
+                    nc.sync.dma_start(
+                        w4_s[32 * q : 32 * q + 4, :].bitcast(I32).rearrange("r (b c) -> r b c", b=2),
+                        w4_scales[:, 4 * q : 4 * q + 4, :].bitcast(I32).rearrange("b r c -> r b c"),
+                    )
             if i in (2, 4, 6):
                 add_foam(i // 2 - 1)
+            if i in (2, 4):
+                foam_t[i // 2 + 1] = load_foam(i // 2 + 1)
             if i == 4:
                 turn_back_first()
                 nc.vector.quantize_mx(out=z_c0[:].bitcast(FP8X4), scales=z_s0[:], in_=z_bf0[:])
         turn_back_second()
+        w4_w = keep.tile([P, 2 * 2 * N], U8, name="w4_w", tag="z_turned1_0", align_bytes=64)
+        nc.sync.dma_start(
+            w4_w[:].bitcast(I32).rearrange("p (b c) -> p b c", b=2), w4_words.bitcast(I32).rearrange("b p c -> p b c")
+        )
 
         def passes(sums, b, codes, scales):
             for nt in range(3):

@@ -20,7 +20,7 @@ ACT = mybir.ActivationFunctionType
 P = 128
 PAGES = 3
 H_RING = 3
-X_RING = 4
+X_RING = 6
 PIECES = (256, 256, 256, 128, 128)
 
 
@@ -43,7 +43,7 @@ def tile_list_spring_fatigue_features_kernel(
         offs3_t = lists.tile([P, M // 16], U16, name="offs3_t")
 
         tab_s = keep.tile([P, T // 4], I32, name="tab_s", tag="slot_d", align_bytes=64)
-        pages = [keep.tile([P, T2], F32, name="page0", align_bytes=64)]
+        pages = [keep.tile([P, T2], F32, name=f"page{k}", align_bytes=64) for k in range(PAGES)]
         nc.vector.memset(tab_s[:], 0)
         ident_made = early.tile([P, P], F32, name="ident_made", align_bytes=64, offset=4 * T - 256)
         ident = keep.tile([P, P], F32, name="ident", align_bytes=64)
@@ -97,32 +97,37 @@ def tile_list_spring_fatigue_features_kernel(
 
         w1_raw1 = keep.tile([P, 4, 512], F32, name="w1_raw1", tag="slot_b", align_bytes=64)
         wgt_t = keep.tile([P, M], F32, name="wgt_t", tag="slot_d", align_bytes=64)
-        for k in range(1, PAGES):
-            page = early.tile([P, T2], F32, name=f"page{k}", align_bytes=64, offset=4 * T2 * (k - 1))
-            nc.gpsimd.memset(page[:], 0.0)
-            pages.append(page)
         nc.sync.dma_start(w1_raw1[:], w1_rows[:, :, 512:1024])
         nc.sync.dma_start(wgt_t[:], wgt)
+        w5_raw = early.tile([P, 2, 4, N], F32, name="w5_raw", align_bytes=64, offset=0)
+        nc.sync.dma_start(w5_raw[:], w5.rearrange("(b p j) n -> p b j n", b=2, j=4))
 
         work = keep.tile([P, X_RING, S], F32, name="work", align_bytes=64)
-        h_t = [keep.tile([P, S], F32, name=f"h{k}") for k in range(H_RING)]
+        h_t = {}
         gw_t = [keep.tile([P, S], F32, name=f"gw{k}") for k in range(H_RING)]
 
-        first_gw = keep.tile([P, 256], F32, name="first_gw")
+        gw_of = {}
+        for i, tag in enumerate(("slot_e", "slot_f")):
+            gw_of[i] = keep.tile([P, S], F32, name=f"gw_first{i}", tag=tag, align_bytes=64)
+
+        def gain_product(i, lo, hi):
+            nc.vector.tensor_scalar_mul(gw_of[i][:, lo:hi], wgs_t[:, lo:hi], gain_t[:, 0, i : i + 1])
 
         def features(i, spans):
             b, t = divmod(i, 4)
-            a = work[:, (i - 1) % X_RING, :]
-            gw = gw_t[i % H_RING]
-            factor = gain_t[:, b, t : t + 1]
+            a = work[:, max(i - 1, 0) % X_RING, :]
+            ahead = i in gw_of
+            if not ahead:
+                gw_of[i] = gw_t[i % H_RING]
+            size = a if ahead else gw_of[i][:]
+            if i == 0:
+                a = gw_of[1][:]
+            h_t[i] = keep.tile([P, S], F32, name=f"h{i}", tag=f"h{i % H_RING}", align_bytes=64)
             for n, (lo, hi) in enumerate(spans):
-                ahead = (i, n) == (0, 0)
-                if ahead:
-                    nc.scalar.activation(first_gw[:], wgs_t[:, lo:hi], ACT.Copy, scale=factor)
                 for c0 in range(lo, hi, 512):
                     c1 = min(hi, c0 + 512)
                     half, v0 = divmod(c0, 512)
-                    load = bank(n if i == 0 else half)
+                    load = bank(2 + n if i == 0 else 6 * (i % 2) + half)
                     nc.tensor.matmul_mx(
                         out=load[:, 0 : c1 - c0],
                         lhsT=w1_c[b][:, P * t : P * (t + 1)].bitcast(FP8X4),
@@ -132,18 +137,18 @@ def tile_list_spring_fatigue_features_kernel(
                         start=True,
                         stop=True,
                     )
-                    nc.scalar.activation(gw[:, c0:c1], load[:, 0 : c1 - c0], ACT.Abs)
-                nc.scalar.activation(a[:, lo:hi], gw[:, lo:hi], ACT.Square, bias=1.0)
-                nc.scalar.activation(h_t[i % H_RING][:, lo:hi], a[:, lo:hi], ACT.Abs_reciprocal_sqrt)
+                    nc.scalar.activation(size[:, c0:c1], load[:, 0 : c1 - c0], ACT.Abs)
+                nc.scalar.activation(a[:, lo:hi], size[:, lo:hi], ACT.Square, bias=1.0)
                 if not ahead:
-                    nc.scalar.activation(gw[:, lo:hi], wgs_t[:, lo:hi], ACT.Copy, scale=factor)
+                    nc.scalar.activation(size[:, lo:hi], wgs_t[:, lo:hi], ACT.Copy, scale=gain_t[:, b, t : t + 1])
+                nc.scalar.activation(h_t[i][:, lo:hi], a[:, lo:hi], ACT.Abs_reciprocal_sqrt)
 
         def scatter(i, spans):
-            for n, (lo, hi) in enumerate(spans):
+            for lo, hi in spans:
                 nc.vector.tensor_tensor(
                     pages[i % PAGES][:].indirect(offs2_t[:, lo // 16 : hi // 16]),
-                    h_t[i % H_RING][:, lo:hi],
-                    first_gw[:] if (i, n) == (0, 0) else gw_t[i % H_RING][:, lo:hi],
+                    h_t[i][:, lo:hi],
+                    gw_of[i][:, lo:hi],
                     ALU.mult,
                 )
 
@@ -183,12 +188,11 @@ def tile_list_spring_fatigue_features_kernel(
                 )
 
         z_bf0 = keep.tile([P, 4 * M], BF16, name="z_bf0", align_bytes=64)
-        z_c0 = keep.tile([P, M], U32, name="z_c0", align_bytes=64)
         z_s0 = keep.tile([P, M], U8, name="z_s0", align_bytes=64)
 
         def turn_back_first():
             for k in range(4):
-                acc = bank(6 + k % 2)
+                acc = bank(2 + k)
                 for u in range(2):
                     for c in range(2):
                         col = 256 * u + P * c
@@ -207,7 +211,7 @@ def tile_list_spring_fatigue_features_kernel(
 
         def turn_back_second():
             for k2 in range(2):
-                acc = bank(6 + k2)
+                acc = bank(k2)
                 for c in range(4):
                     k, cc = divmod(4 * k2 + c, 2)
                     nc.tensor.transpose(
@@ -218,11 +222,11 @@ def tile_list_spring_fatigue_features_kernel(
                         lo = starts[n] - 512 * k2
                         nc.scalar.copy(z_pairs[n][:].bitcast(F32)[:, 0:w], acc[:, lo : lo + w])
 
-        w5_bf = keep.tile([P, 2 * 4 * N], BF16, name="w5_bf", tag="slot_f", align_bytes=64)
         w5_c = keep.tile([P, 2 * N], U32, name="w5_c", align_bytes=64)
         w5_s = keep.tile([P, 2 * N], U8, name="w5_s", align_bytes=64)
 
         def prepare_w5():
+            w5_bf = keep.tile([P, 2 * 4 * N], BF16, name="w5_bf", tag="slot_f", align_bytes=64)
             for b in range(2):
                 nc.scalar.copy(
                     w5_bf[:, 4 * N * b : 4 * N * (b + 1)].rearrange("p (n j) -> p n j", j=4),
@@ -235,21 +239,27 @@ def tile_list_spring_fatigue_features_kernel(
 
         whole = [(0, S)]
         halves = [(0, 256), (256, 512), (512, S)]
+        gain_product(0, 0, S)
         features(0, halves)
-        scatter(0, halves)
+        scatter(0, halves[0:1])
+        gain_product(1, 0, 512)
+        scatter(0, halves[1:2])
+        gain_product(1, 512, S)
+        scatter(0, halves[2:3])
         features(1, whole)
-        prepare_w1(1, w1_raw1, nc.scalar.copy, "slot_e")
-        foam_t = {0: load_foam(0)}
-        w5_raw = keep.tile([P, 2, 4, N], F32, name="w5_raw", tag="slot_e", align_bytes=64)
-        nc.sync.dma_start(w5_raw[:], w5.rearrange("(b p j) n -> p b j n", b=2, j=4))
+        foam_t = {}
         for i in range(7):
             scatter(i + 1, whole)
-            gather(i, 0, M)
+            if i < 6:
+                gather(i, 0, M)
             if i + 2 < 8:
                 features(i + 2, whole)
+            if i == 0:
+                prepare_w1(1, w1_raw1, nc.scalar.copy, "slot_e")
+                foam_t[0] = load_foam(0)
+                foam_t[1] = load_foam(1)
             if i == 1:
                 prepare_w5()
-                foam_t[1] = load_foam(1)
                 w4_s = keep.tile([P, 2 * N], U8, name="w4_s", tag="slot_f", align_bytes=64)
                 nc.vector.memset(w4_s[:].bitcast(I32), 0)
                 for q in range(4):
@@ -257,14 +267,15 @@ def tile_list_spring_fatigue_features_kernel(
                         w4_s[32 * q : 32 * q + 4, :].bitcast(I32).rearrange("r (b c) -> r b c", b=2),
                         w4_scales[:, 4 * q : 4 * q + 4, :].bitcast(I32).rearrange("b r c -> r b c"),
                     )
-            if i in (2, 4, 6):
+            if i in (3, 5):
                 add_foam(i // 2 - 1)
-            if i in (2, 4):
                 foam_t[i // 2 + 1] = load_foam(i // 2 + 1)
-            if i == 4:
+            if i == 5:
                 turn_back_first()
-                nc.vector.quantize_mx(out=z_c0[:].bitcast(FP8X4), scales=z_s0[:], in_=z_bf0[:])
+        add_foam(2)
         turn_back_second()
+        z_c0 = keep.tile([P, M], U32, name="z_c0", tag=f"h{7 % H_RING}", align_bytes=64)
+        nc.vector.quantize_mx(out=z_c0[:].bitcast(FP8X4), scales=z_s0[:], in_=z_bf0[:])
         w4_w = keep.tile([P, 2 * 2 * N], U8, name="w4_w", tag="z_turned1_0", align_bytes=64)
         nc.sync.dma_start(
             w4_w[:].bitcast(I32).rearrange("p (b c) -> p b c", b=2), w4_words.bitcast(I32).rearrange("b p c -> p b c")
@@ -303,10 +314,12 @@ def tile_list_spring_fatigue_features_kernel(
 
         def make_z(n):
             lo, w = starts[n], PIECES[n]
+            if lo % 512 == 0:
+                gather(6, lo, lo + 512)
             gather(7, lo, lo + w)
             nc.vector.tensor_tensor(
                 z_pairs[n][:, 2 * w : 4 * w].rearrange("p (c i e) -> p c e i", i=4, e=2),
-                work[:, 2:4, lo : lo + w].rearrange("p e (c i) -> p c e i", i=4),
+                work[:, 0:2, lo : lo + w].rearrange("p e (c i) -> p c e i", i=4),
                 foam_t[3][:, :, lo : lo + w].rearrange("p e (c i) -> p c e i", i=4),
                 ALU.add,
             )

@@ -18,10 +18,16 @@ ALU = mybir.AluOpType
 ACT = mybir.ActivationFunctionType
 
 P = 128
+BANK = 512
+BANKS = 8
+PLANES = 8
+LAST = PLANES - 1
+N_TILES = N // P
 PAGES = 3
 H_RING = 3
 X_RING = 6
-PIECES = (256, 256, 256, 128, 128)
+FIRST_PIECES = ((0, 256), (256, 512), (512, S))
+LAST_PIECES = ((0, 256), (256, 512), (512, 768), (768, 896), (896, M))
 
 
 def tile_list_spring_fatigue_features_kernel(
@@ -31,21 +37,22 @@ def tile_list_spring_fatigue_features_kernel(
     with ExitStack() as ctx:
         lists = ctx.enter_context(tc.tile_pool(name="lists", bufs=1))
         keep = ctx.enter_context(tc.tile_pool(name="keep", bufs=1))
-        early = ctx.enter_context(tc.tile_pool(name="early", bufs=1))
+        placed = ctx.enter_context(tc.tile_pool(name="placed", bufs=1))
         ring = ctx.enter_context(tc.tile_pool(name="ring", bufs=3))
         psum = ctx.enter_context(tc.psum_pool(name="psum", bufs=1))
 
         def bank(k):
-            return psum.tile([P, 512], F32, name=f"bank{k}", tag=f"bank{k}")
+            return psum.tile([P, BANK], F32, name=f"bank{k}", tag=f"bank{k}")
 
         offs_t = lists.tile([P, S // 16], U16, name="offs_t")
         offs2_t = lists.tile([P, S // 16], U16, name="offs2_t")
         offs3_t = lists.tile([P, M // 16], U16, name="offs3_t")
 
-        tab_s = keep.tile([P, T // 4], I32, name="tab_s", tag="slot_d", align_bytes=64)
+        tab_s = keep.tile([P, T // 4], I32, name="tab_s", tag="chain_d", align_bytes=64)
         pages = [keep.tile([P, T2], F32, name=f"page{k}", align_bytes=64) for k in range(PAGES)]
         nc.vector.memset(tab_s[:], 0)
-        ident_made = early.tile([P, P], F32, name="ident_made", align_bytes=64, offset=4 * T - 256)
+        table_bytes = 4 * T
+        ident_made = placed.tile([P, P], F32, name="ident_made", align_bytes=64, offset=table_bytes - 2 * P)
         ident = keep.tile([P, P], F32, name="ident", align_bytes=64)
         make_identity(nc, ident_made[:])
         nc.gpsimd.tensor_copy(ident[:], ident_made[:])
@@ -56,77 +63,81 @@ def tile_list_spring_fatigue_features_kernel(
 
         w1_rows = w1.rearrange("(p j) c -> p j c", j=4)
         foam_rows = foam.rearrange("(b p u e) m -> b u p e m", b=2, u=2, e=2)
-        gain_t = keep.tile([P, 2, 4], F32, name="gain_t")
-        w1_raw0 = keep.tile([P, 4, 512], F32, name="w1_raw0", tag="slot_a", align_bytes=64)
-        tab_w = early.tile([P, T], U32, name="tab_w", align_bytes=64, offset=0)
+        gain_t = placed.tile([P, 2, 4], F32, name="gain_t", align_bytes=64, offset=table_bytes)
+        w1_raw0 = keep.tile([P, 4, BANK], F32, name="w1_raw0", align_bytes=64)
+        tab_w = placed.tile([P, T], U32, name="tab_w", align_bytes=64, offset=0)
         nc.sync.dma_start(offs_t[:], offs)
-        nc.sync.dma_start(w1_raw0[:], w1_rows[:, :, 0:512])
-        for q in range(4):
+        nc.sync.dma_start(w1_raw0[:], w1_rows[:, :, 0:BANK])
+        for quad in range(4):
             nc.sync.dma_start(
-                tab_s[32 * q : 32 * q + 4, :], tab_scales[0, 4 * q : 4 * q + 4, :].bitcast(I32)
+                tab_s[32 * quad : 32 * quad + 4, :], tab_scales[0, 4 * quad : 4 * quad + 4, :].bitcast(I32)
             )
         nc.sync.dma_start(tab_w[:].bitcast(I32), tab_words[0].rearrange("p t i -> p (t i)").bitcast(I32))
-        wgs_t = early.tile([P, S], F32, name="wgs_t", align_bytes=64, offset=4 * T)
-        nc.sync.dma_start(wgs_t[:], wgs)
+        wgs_t = placed.tile([P, S], F32, name="wgs_t", align_bytes=64, offset=table_bytes + 64)
         nc.sync.dma_start(gain_t[:], gain.rearrange("(b p t) -> p b t", b=2, t=4))
+        nc.sync.dma_start(wgs_t[:], wgs)
         nc.sync.dma_start(offs2_t[:], offs2)
         nc.sync.dma_start(offs3_t[:], offs3)
 
         def load_foam(pair):
-            tile = keep.tile([P, 2, M], F32, name=f"foam{pair}", tag=("slot_b", "slot_e")[pair % 2], align_bytes=64)
+            tile = keep.tile([P, 2, M], F32, name=f"foam{pair}", tag=("chain_a", "chain_b")[pair % 2], align_bytes=64)
             nc.sync.dma_start(tile[:], foam_rows[pair // 2, pair % 2])
             return tile
 
-        w1_c = [keep.tile([P, 512], U32, name=f"w1_c{b}", align_bytes=64) for b in range(2)]
-        w1_s = [keep.tile([P, 512], U8, name=f"w1_s{b}", align_bytes=64) for b in range(2)]
+        w1_c = [keep.tile([P, BANK], U32, name=f"w1_c{b}", align_bytes=64) for b in range(2)]
+        w1_s = [keep.tile([P, BANK], U8, name=f"w1_s{b}", align_bytes=64) for b in range(2)]
 
-        def prepare_w1(b, raw, copy, tag):
-            rounded = keep.tile([P, 2048], BF16, name=f"w1_bf{b}", tag=tag, align_bytes=64)
-            copy(
-                rounded[:].rearrange("p (t m j) -> p m t j", t=4, j=4),
-                raw[:].rearrange("p j (m t) -> p m t j", t=4),
+        def prepare_w1(b, raw, tag):
+            rounded = keep.tile([P, 4 * BANK], BF16, name=f"w1_bf{b}", tag=tag, align_bytes=64)
+            nc.scalar.copy(
+                rounded[:].rearrange("p (t c j) -> p c t j", t=4, j=4),
+                raw[:].rearrange("p j (c t) -> p c t j", t=4),
             )
             nc.vector.quantize_mx(out=w1_c[b][:].bitcast(FP8X4), scales=w1_s[b][:], in_=rounded[:])
 
         v_s = keep.tile([P, S], U8, name="v_s", align_bytes=64)
-        v_w = [keep.tile([P, 512], U32, name=f"v_w{half}", align_bytes=64) for half in range(2)]
+        v_w = [keep.tile([P, BANK], U32, name=f"v_w{half}", align_bytes=64) for half in range(2)]
         nc.vector.tensor_copy(v_s[:], tab_s[:].bitcast(U8).indirect(offs_t[:]))
-        prepare_w1(0, w1_raw0, nc.scalar.copy, "slot_b")
+        prepare_w1(0, w1_raw0, "chain_a")
         for half in range(2):
             nc.vector.tensor_copy(v_w[half][:], tab_w[:].indirect(offs_t[:, 32 * half : 32 * (half + 1)]))
 
-        w1_raw1 = keep.tile([P, 4, 512], F32, name="w1_raw1", tag="slot_b", align_bytes=64)
-        wgt_t = keep.tile([P, M], F32, name="wgt_t", tag="slot_d", align_bytes=64)
-        nc.sync.dma_start(w1_raw1[:], w1_rows[:, :, 512:1024])
+        w1_raw1 = keep.tile([P, 4, BANK], F32, name="w1_raw1", tag="chain_a", align_bytes=64)
+        wgt_t = keep.tile([P, M], F32, name="wgt_t", tag="chain_d", align_bytes=64)
+        nc.sync.dma_start(w1_raw1[:], w1_rows[:, :, BANK:H])
         nc.sync.dma_start(wgt_t[:], wgt)
-        w5_raw = early.tile([P, 2, 4, N], F32, name="w5_raw", align_bytes=64, offset=0)
+        w5_raw = placed.tile([P, 2, 4, N], F32, name="w5_raw", align_bytes=64, offset=0)
         nc.sync.dma_start(w5_raw[:], w5.rearrange("(b p j) n -> p b j n", b=2, j=4))
 
         work = keep.tile([P, X_RING, S], F32, name="work", align_bytes=64)
-        h_t = {}
-        gw_t = [keep.tile([P, S], F32, name=f"gw{k}") for k in range(H_RING)]
-
+        h_of = {}
+        gw_ring = [keep.tile([P, S], F32, name=f"gw{k}") for k in range(H_RING)]
         gw_of = {}
-        for i, tag in enumerate(("slot_e", "slot_f")):
+        for i, tag in enumerate(("chain_b", "chain_c")):
             gw_of[i] = keep.tile([P, S], F32, name=f"gw_first{i}", tag=tag, align_bytes=64)
 
         def gain_product(i, lo, hi):
             nc.vector.tensor_scalar_mul(gw_of[i][:, lo:hi], wgs_t[:, lo:hi], gain_t[:, 0, i : i + 1])
 
-        def features(i, spans):
-            b, t = divmod(i, 4)
-            a = work[:, max(i - 1, 0) % X_RING, :]
-            ahead = i in gw_of
-            if not ahead:
-                gw_of[i] = gw_t[i % H_RING]
-            size = a if ahead else gw_of[i][:]
+        def feature_tiles(i):
             if i == 0:
-                a = gw_of[1][:]
-            h_t[i] = keep.tile([P, S], F32, name=f"h{i}", tag=f"h{i % H_RING}", align_bytes=64)
-            for n, (lo, hi) in enumerate(spans):
-                for c0 in range(lo, hi, 512):
-                    c1 = min(hi, c0 + 512)
-                    half, v0 = divmod(c0, 512)
+                return work[:, 0, :], gw_of[1][:]
+            if i == 1:
+                return work[:, 0, :], work[:, 0, :]
+            gw_of[i] = gw_ring[i % H_RING]
+            return gw_of[i][:], work[:, (i - 1) % X_RING, :]
+
+        def square(i, roots, lo, hi):
+            nc.scalar.activation(h_of[i][:, lo:hi], roots[:, lo:hi], ACT.Square)
+
+        def features(i, pieces):
+            b, t = divmod(i, 4)
+            size, roots = feature_tiles(i)
+            h_of[i] = keep.tile([P, S], F32, name=f"h{i}", tag=f"h{i % H_RING}", align_bytes=64)
+            for n, (lo, hi) in enumerate(pieces):
+                for c0 in range(lo, hi, BANK):
+                    c1 = min(hi, c0 + BANK)
+                    half, v0 = divmod(c0, BANK)
                     load = bank(2 + n if i == 0 else 6 * (i % 2) + half)
                     nc.tensor.matmul_mx(
                         out=load[:, 0 : c1 - c0],
@@ -138,19 +149,20 @@ def tile_list_spring_fatigue_features_kernel(
                         stop=True,
                     )
                     nc.scalar.activation(size[:, c0:c1], load[:, 0 : c1 - c0], ACT.Abs)
-                nc.scalar.activation(a[:, lo:hi], size[:, lo:hi], ACT.Square, bias=1.0)
-                if not ahead:
+                nc.scalar.activation(roots[:, lo:hi], size[:, lo:hi], ACT.Abs_reciprocal_sqrt, bias=1.0)
+                if i >= 2:
                     nc.scalar.activation(size[:, lo:hi], wgs_t[:, lo:hi], ACT.Copy, scale=gain_t[:, b, t : t + 1])
-                nc.scalar.activation(h_t[i][:, lo:hi], a[:, lo:hi], ACT.Abs_reciprocal_sqrt)
+                if i < LAST:
+                    square(i, roots, lo, hi)
+            return roots
 
-        def scatter(i, spans):
-            for lo, hi in spans:
-                nc.vector.tensor_tensor(
-                    pages[i % PAGES][:].indirect(offs2_t[:, lo // 16 : hi // 16]),
-                    h_t[i][:, lo:hi],
-                    gw_of[i][:, lo:hi],
-                    ALU.mult,
-                )
+        def scatter(i, lo, hi):
+            nc.vector.tensor_tensor(
+                pages[i % PAGES][:].indirect(offs2_t[:, lo // 16 : hi // 16]),
+                h_of[i][:, lo:hi],
+                gw_of[i][:, lo:hi],
+                ALU.mult,
+            )
 
         def gather(i, lo, hi):
             nc.vector.tensor_tensor(
@@ -161,130 +173,141 @@ def tile_list_spring_fatigue_features_kernel(
             )
 
         z_turned = [
-            [keep.tile([P, 512], BF16, name=f"z_turned{u}_{k}", align_bytes=64) for k in range(4)] for u in range(2)
+            [keep.tile([P, BANK], BF16, name=f"z_turned{u}_{k}", align_bytes=64) for k in range(4)] for u in range(2)
         ]
+        foam_of = {}
 
         def add_foam(pair):
-            u = pair % 2
+            sources = [foam_of[pair][:, e, :] for e in range(2)]
+            sources = sources + [work[:, (2 * pair + e) % X_RING, :] for e in range(2)]
+            sums = [bank(2 + k) for k in range(4)]
+            for s in range(4):
+                for k in range(4):
+                    for c in range(2):
+                        col = 2 * P * c + P * (s % 2)
+                        m0 = 2 * P * k + P * c
+                        nc.tensor.matmul(
+                            sums[k][:, col : col + P],
+                            sources[s][:, m0 : m0 + P],
+                            ident[:],
+                            start=(s, c) == (0, 0),
+                            stop=(s, c) == (3, 1),
+                            is_transpose=True,
+                        )
             for k in range(4):
-                acc = bank(2 + k)
-                sources = [foam_t[pair][:, e, :] for e in range(2)]
-                sources = sources + [work[:, (2 * pair + e) % X_RING, :] for e in range(2)]
-                steps = [(s, c) for s in range(4) for c in range(2)]
-                for n, (s, c) in enumerate(steps):
-                    col = 256 * c + P * (s % 2)
-                    m0 = 256 * k + P * c
-                    nc.tensor.matmul(
-                        acc[:, col : col + P],
-                        sources[s][:, m0 : m0 + P],
-                        ident[:],
-                        start=(n == 0),
-                        stop=(n == len(steps) - 1),
-                        is_transpose=True,
-                    )
                 nc.scalar.copy(
-                    z_turned[u][k][:].rearrange("m (c p e) -> m c p e", c=2, e=2),
-                    acc[:].rearrange("m (c e p) -> m c p e", c=2, e=2),
+                    z_turned[pair % 2][k][:].rearrange("m (c p e) -> m c p e", c=2, e=2),
+                    sums[k][:].rearrange("m (c e p) -> m c p e", c=2, e=2),
                 )
 
-        z_bf0 = keep.tile([P, 4 * M], BF16, name="z_bf0", align_bytes=64)
+        z_bf = keep.tile([P, 4 * M], BF16, name="z_bf", align_bytes=64)
         z_s0 = keep.tile([P, M], U8, name="z_s0", align_bytes=64)
 
-        def turn_back_first():
+        def turn_back_pass0():
             for k in range(4):
-                acc = bank(2 + k)
+                words = bank(2 + k)
                 for u in range(2):
                     for c in range(2):
-                        col = 256 * u + P * c
+                        col = 2 * P * u + P * c
                         nc.tensor.transpose(
-                            acc[:, col : col + P], z_turned[u][k][:].bitcast(F32)[:, P * c : P * (c + 1)], ident[:]
+                            words[:, col : col + P], z_turned[u][k][:].bitcast(F32)[:, P * c : P * (c + 1)], ident[:]
                         )
                 nc.scalar.copy(
-                    z_bf0[:].bitcast(F32)[:, 512 * k : 512 * (k + 1)].rearrange("p (m u) -> p m u", u=2),
-                    acc[:].rearrange("p (u m) -> p m u", u=2),
+                    z_bf[:].bitcast(F32)[:, BANK * k : BANK * (k + 1)].rearrange("p (m u) -> p m u", u=2),
+                    words[:].rearrange("p (u m) -> p m u", u=2),
                 )
 
-        starts = [sum(PIECES[:n]) for n in range(len(PIECES))]
         z_pairs = [
-            keep.tile([P, 4 * w], BF16, name=f"z_pairs{n}", align_bytes=64) for n, w in enumerate(PIECES)
+            keep.tile([P, 4 * (hi - lo)], BF16, name=f"z_pairs{n}", align_bytes=64)
+            for n, (lo, hi) in enumerate(LAST_PIECES)
         ]
 
-        def turn_back_second():
-            for k2 in range(2):
-                acc = bank(k2)
-                for c in range(4):
-                    k, cc = divmod(4 * k2 + c, 2)
+        def turn_back_planes_4_5():
+            for half in range(2):
+                words = bank(half)
+                for chunk in range(4):
+                    k, c = divmod(4 * half + chunk, 2)
                     nc.tensor.transpose(
-                        acc[:, P * c : P * (c + 1)], z_turned[0][k][:].bitcast(F32)[:, P * cc : P * (cc + 1)], ident[:]
+                        words[:, P * chunk : P * (chunk + 1)],
+                        z_turned[0][k][:].bitcast(F32)[:, P * c : P * (c + 1)],
+                        ident[:],
                     )
-                for n, w in enumerate(PIECES):
-                    if starts[n] // 512 == k2:
-                        lo = starts[n] - 512 * k2
-                        nc.scalar.copy(z_pairs[n][:].bitcast(F32)[:, 0:w], acc[:, lo : lo + w])
+                for n, (lo, hi) in enumerate(LAST_PIECES):
+                    if lo // BANK == half:
+                        nc.scalar.copy(
+                            z_pairs[n][:].bitcast(F32)[:, 0 : hi - lo], words[:, lo - BANK * half : hi - BANK * half]
+                        )
 
         w5_c = keep.tile([P, 2 * N], U32, name="w5_c", align_bytes=64)
         w5_s = keep.tile([P, 2 * N], U8, name="w5_s", align_bytes=64)
 
         def prepare_w5():
-            w5_bf = keep.tile([P, 2 * 4 * N], BF16, name="w5_bf", tag="slot_f", align_bytes=64)
+            rounded = keep.tile([P, 2 * 4 * N], BF16, name="w5_bf", tag="chain_c", align_bytes=64)
             for b in range(2):
                 nc.scalar.copy(
-                    w5_bf[:, 4 * N * b : 4 * N * (b + 1)].rearrange("p (n j) -> p n j", j=4),
+                    rounded[:, 4 * N * b : 4 * N * (b + 1)].rearrange("p (n j) -> p n j", j=4),
                     w5_raw[:, b].rearrange("p j n -> p n j"),
                 )
-            for lo, hi in ((0, 512), (512, 768)):
+            for lo, hi in ((0, BANK), (BANK, 2 * N)):
                 nc.vector.quantize_mx(
-                    out=w5_c[:, lo:hi].bitcast(FP8X4), scales=w5_s[:, lo:hi], in_=w5_bf[:, 4 * lo : 4 * hi]
+                    out=w5_c[:, lo:hi].bitcast(FP8X4), scales=w5_s[:, lo:hi], in_=rounded[:, 4 * lo : 4 * hi]
                 )
 
-        whole = [(0, S)]
-        halves = [(0, 256), (256, 512), (512, S)]
+        def load_w4_scales():
+            tile = keep.tile([P, 2 * N], U8, name="w4_s", tag="chain_c", align_bytes=64)
+            nc.vector.memset(tile[:].bitcast(I32), 0)
+            for quad in range(4):
+                nc.sync.dma_start(
+                    tile[32 * quad : 32 * quad + 4, :].bitcast(I32).rearrange("r (b c) -> r b c", b=2),
+                    w4_scales[:, 4 * quad : 4 * quad + 4, :].bitcast(I32).rearrange("b r c -> r b c"),
+                )
+            return tile
+
         gain_product(0, 0, S)
-        features(0, halves)
-        scatter(0, halves[0:1])
-        gain_product(1, 0, 512)
-        scatter(0, halves[1:2])
-        gain_product(1, 512, S)
-        scatter(0, halves[2:3])
-        features(1, whole)
-        foam_t = {}
-        for i in range(7):
-            scatter(i + 1, whole)
-            if i < 6:
-                gather(i, 0, M)
-            if i + 2 < 8:
-                features(i + 2, whole)
-            if i == 0:
-                prepare_w1(1, w1_raw1, nc.scalar.copy, "slot_e")
-                foam_t[0] = load_foam(0)
-                foam_t[1] = load_foam(1)
-            if i == 1:
-                prepare_w5()
-                w4_s = keep.tile([P, 2 * N], U8, name="w4_s", tag="slot_f", align_bytes=64)
-                nc.vector.memset(w4_s[:].bitcast(I32), 0)
-                for q in range(4):
-                    nc.sync.dma_start(
-                        w4_s[32 * q : 32 * q + 4, :].bitcast(I32).rearrange("r (b c) -> r b c", b=2),
-                        w4_scales[:, 4 * q : 4 * q + 4, :].bitcast(I32).rearrange("b r c -> r b c"),
-                    )
-            if i in (3, 5):
-                add_foam(i // 2 - 1)
-                foam_t[i // 2 + 1] = load_foam(i // 2 + 1)
-            if i == 5:
-                turn_back_first()
+        features(0, FIRST_PIECES)
+        scatter(0, *FIRST_PIECES[0])
+        gain_product(1, 0, BANK)
+        scatter(0, *FIRST_PIECES[1])
+        gain_product(1, BANK, S)
+        scatter(0, *FIRST_PIECES[2])
+        features(1, [(0, S)])
+
+        def step(i):
+            scatter(i + 1, 0, S)
+            gather(i, 0, M)
+            return features(i + 2, [(0, S)])
+
+        step(0)
+        prepare_w1(1, w1_raw1, "chain_b")
+        foam_of[0] = load_foam(0)
+        foam_of[1] = load_foam(1)
+        step(1)
+        prepare_w5()
+        w4_s = load_w4_scales()
+        step(2)
+        step(3)
+        add_foam(0)
+        foam_of[2] = load_foam(2)
+        step(4)
+        last_roots = step(5)
+        add_foam(1)
+        foam_of[3] = load_foam(3)
+        turn_back_pass0()
+        square(LAST, last_roots, 0, S)
+        scatter(LAST, 0, S)
         add_foam(2)
-        turn_back_second()
-        z_c0 = keep.tile([P, M], U32, name="z_c0", tag=f"h{7 % H_RING}", align_bytes=64)
-        nc.vector.quantize_mx(out=z_c0[:].bitcast(FP8X4), scales=z_s0[:], in_=z_bf0[:])
+        turn_back_planes_4_5()
+        z_c0 = keep.tile([P, M], U32, name="z_c0", tag=f"h{LAST % H_RING}", align_bytes=64)
+        nc.vector.quantize_mx(out=z_c0[:].bitcast(FP8X4), scales=z_s0[:], in_=z_bf[:])
         w4_w = keep.tile([P, 2 * 2 * N], U8, name="w4_w", tag="z_turned1_0", align_bytes=64)
         nc.sync.dma_start(
             w4_w[:].bitcast(I32).rearrange("p (b c) -> p b c", b=2), w4_words.bitcast(I32).rearrange("b p c -> p b c")
         )
 
         def passes(sums, b, codes, scales):
-            for nt in range(3):
+            for nt in range(N_TILES):
                 col = N * b + P * nt
-                flags = dict(start=(b == 0 and nt == 0), stop=(b == 1 and nt == 2))
+                flags = dict(start=(b == 0 and nt == 0), stop=(b == 1 and nt == N_TILES - 1))
                 nc.tensor.matmul_mx(
                     out=sums[0][:, P * nt : P * (nt + 1)],
                     lhsT=w4_w[:, 2 * col : 2 * (col + P)].bitcast(FP4X4),
@@ -303,45 +326,44 @@ def tile_list_spring_fatigue_features_kernel(
                 )
 
         def open_sums(chunk):
-            sums = (bank(2 * chunk % 8), bank((2 * chunk + 1) % 8))
+            sums = (bank(2 * chunk % BANKS), bank((2 * chunk + 1) % BANKS))
             cols = slice(P * chunk, P * (chunk + 1))
             passes(sums, 0, z_c0[:, cols], z_s0[:, cols])
             return sums
 
-        opened = {chunk: open_sums(chunk) for chunk in range(4)}
+        opened = {chunk: open_sums(chunk) for chunk in range(BANKS // 2)}
         out_rows = out.rearrange("(nt p) m -> p nt m", p=P)
         quantised = {}
 
         def make_z(n):
-            lo, w = starts[n], PIECES[n]
-            if lo % 512 == 0:
-                gather(6, lo, lo + 512)
-            gather(7, lo, lo + w)
+            lo, hi = LAST_PIECES[n]
+            width = hi - lo
+            if lo % BANK == 0:
+                gather(LAST - 1, lo, lo + BANK)
+            gather(LAST, lo, hi)
             nc.vector.tensor_tensor(
-                z_pairs[n][:, 2 * w : 4 * w].rearrange("p (c i e) -> p c e i", i=4, e=2),
-                work[:, 0:2, lo : lo + w].rearrange("p e (c i) -> p c e i", i=4),
-                foam_t[3][:, :, lo : lo + w].rearrange("p e (c i) -> p c e i", i=4),
+                z_pairs[n][:, 2 * width : 4 * width].rearrange("p (c i e) -> p c e i", i=4, e=2),
+                work[:, 0:2, lo:hi].rearrange("p e (c i) -> p c e i", i=4),
+                foam_of[3][:, :, lo:hi].rearrange("p e (c i) -> p c e i", i=4),
                 ALU.add,
             )
-            z_bf = z_bf0[:, 4 * lo : 4 * (lo + w)]
             nc.scalar.copy(
-                z_bf0[:].bitcast(F32)[:, 2 * lo : 2 * (lo + w)].rearrange("p (m u) -> p m u", u=2),
+                z_bf[:].bitcast(F32)[:, 2 * lo : 2 * hi].rearrange("p (m u) -> p m u", u=2),
                 z_pairs[n][:].bitcast(F32).rearrange("p (u m) -> p m u", u=2),
             )
-            quantised[n] = z_bf
 
         def quantise_z(n):
-            w = PIECES[n]
-            z_c = keep.tile([P, w], U32, name=f"z_c1_{n}", align_bytes=64)
-            z_s = keep.tile([P, w], U8, name=f"z_s1_{n}", align_bytes=64)
-            nc.vector.quantize_mx(out=z_c[:].bitcast(FP8X4), scales=z_s[:], in_=quantised[n])
+            lo, hi = LAST_PIECES[n]
+            z_c = keep.tile([P, hi - lo], U32, name=f"z_c1_{n}", align_bytes=64)
+            z_s = keep.tile([P, hi - lo], U8, name=f"z_s1_{n}", align_bytes=64)
+            nc.vector.quantize_mx(out=z_c[:].bitcast(FP8X4), scales=z_s[:], in_=z_bf[:, 4 * lo : 4 * hi])
             quantised[n] = (z_c, z_s)
 
         def finish(n):
-            lo, w = starts[n], PIECES[n]
+            lo, hi = LAST_PIECES[n]
             z_c, z_s = quantised[n]
-            result = keep.tile([P, 3, w], F32, name=f"result{n}")
-            for c in range(w // P):
+            result = keep.tile([P, N_TILES, hi - lo], F32, name=f"result{n}")
+            for c in range((hi - lo) // P):
                 chunk = lo // P + c
                 sums = opened[chunk] if chunk in opened else open_sums(chunk)
                 cols = slice(P * c, P * (c + 1))
@@ -350,17 +372,17 @@ def tile_list_spring_fatigue_features_kernel(
                 nc.scalar.activation(wear[:], sums[0][:, 0:N], ACT.Abs)
                 nc.vector.tensor_tensor(
                     result[:, :, cols],
-                    wear[:].rearrange("p (nt m) -> p nt m", nt=3),
-                    sums[1][:, 0:N].rearrange("p (nt m) -> p nt m", nt=3),
+                    wear[:].rearrange("p (nt m) -> p nt m", nt=N_TILES),
+                    sums[1][:, 0:N].rearrange("p (nt m) -> p nt m", nt=N_TILES),
                     ALU.subtract,
                 )
-            nc.sync.dma_start(out_rows[:, :, lo : lo + w], result[:])
+            nc.sync.dma_start(out_rows[:, :, lo:hi], result[:])
 
-        count = len(PIECES)
-        for step in range(count + 2):
-            if step < count:
-                make_z(step)
-            if 1 <= step <= count:
-                quantise_z(step - 1)
-            if step >= 2:
-                finish(step - 2)
+        count = len(LAST_PIECES)
+        for n in range(count + 2):
+            if n < count:
+                make_z(n)
+            if 1 <= n <= count:
+                quantise_z(n - 1)
+            if n >= 2:
+                finish(n - 2)

from contextlib import ExitStack

import concourse.mybir as mybir
from concourse.masks import make_identity

K, H, N, T, S, M, T2 = 512, 1024, 384, 4096, 1024, 1024, 2048
FLOPS = 2 * K * H * S + 2 * 2 * H * N * M

F32 = mybir.dt.float32
BF16 = mybir.dt.bfloat16
I32 = mybir.dt.int32
U32 = mybir.dt.uint32
U16 = mybir.dt.uint16
U8 = mybir.dt.uint8
FP8X4 = mybir.dt.float8_e4m3fn_x4
FP4X4 = mybir.dt.float4_e2m1fn_x4
ALU = mybir.AluOpType
ACT = mybir.ActivationFunctionType

P = 128
BANK = 512
BANKS = 8
PLANES = 8
LAST = PLANES - 1
N_TILES = N // P
PAGES = 3
H_RING = 3
X_RING = 6
FIRST_PIECES = ((0, 256), (256, 512), (512, S))
LAST_PIECES = ((0, 256), (256, 512), (512, 768), (768, 896), (896, M))


def tile_list_spring_fatigue_features_kernel(
    tc, tab_words, tab_scales, offs, offs2, offs3, w1, gain, wgs, wgt, foam, w4_words, w4_scales, w5, out
):
    nc = tc.nc
    with ExitStack() as ctx:
        lists = ctx.enter_context(tc.tile_pool(name="lists", bufs=1))
        keep = ctx.enter_context(tc.tile_pool(name="keep", bufs=1))
        placed = ctx.enter_context(tc.tile_pool(name="placed", bufs=1))
        ring = ctx.enter_context(tc.tile_pool(name="ring", bufs=3))
        psum = ctx.enter_context(tc.psum_pool(name="psum", bufs=1))

        def bank(k):
            return psum.tile([P, BANK], F32, name=f"bank{k}", tag=f"bank{k}")

        offs_t = lists.tile([P, S // 16], U16, name="offs_t")
        offs2_t = lists.tile([P, S // 16], U16, name="offs2_t")
        offs3_t = lists.tile([P, M // 16], U16, name="offs3_t")

        tab_s = keep.tile([P, T // 4], I32, name="tab_s", tag="chain_d", align_bytes=64)
        pages = [keep.tile([P, T2], F32, name=f"page{k}", align_bytes=64) for k in range(PAGES)]
        nc.vector.memset(tab_s[:], 0)
        table_bytes = 4 * T
        ident_made = placed.tile([P, P], F32, name="ident_made", align_bytes=64, offset=table_bytes - 2 * P)
        ident = keep.tile([P, P], F32, name="ident", align_bytes=64)
        make_identity(nc, ident_made[:])
        nc.gpsimd.tensor_copy(ident[:], ident_made[:])
        for page in pages:
            nc.vector.memset(page[:].bitcast(I32), 0)
        warm = keep.tile([P, 1], F32, name="warm")
        nc.scalar.activation(warm[:], ident[:, 0:1], ACT.Abs_reciprocal_sqrt, bias=1.0)

        w1_rows = w1.rearrange("(p j) c -> p j c", j=4)
        foam_rows = foam.rearrange("(b p u e) m -> b u p e m", b=2, u=2, e=2)
        gain_t = placed.tile([P, 2, 4], F32, name="gain_t", align_bytes=64, offset=table_bytes)
        w1_raw0 = keep.tile([P, 4, BANK], F32, name="w1_raw0", align_bytes=64)
        tab_w = placed.tile([P, T], U32, name="tab_w", align_bytes=64, offset=0)
        nc.sync.dma_start(offs_t[:], offs)
        nc.sync.dma_start(w1_raw0[:], w1_rows[:, :, 0:BANK])
        for quad in range(4):
            nc.sync.dma_start(
                tab_s[32 * quad : 32 * quad + 4, :], tab_scales[0, 4 * quad : 4 * quad + 4, :].bitcast(I32)
            )
        nc.sync.dma_start(tab_w[:].bitcast(I32), tab_words[0].rearrange("p t i -> p (t i)").bitcast(I32))
        wgs_t = placed.tile([P, S], F32, name="wgs_t", align_bytes=64, offset=table_bytes + 64)
        nc.sync.dma_start(gain_t[:], gain.rearrange("(b p t) -> p b t", b=2, t=4))
        nc.sync.dma_start(wgs_t[:], wgs)
        nc.sync.dma_start(offs2_t[:], offs2)
        nc.sync.dma_start(offs3_t[:], offs3)

        def load_foam(pair):
            tile = keep.tile([P, 2, M], F32, name=f"foam{pair}", tag=("chain_a", "chain_b")[pair % 2], align_bytes=64)
            nc.sync.dma_start(tile[:], foam_rows[pair // 2, pair % 2])
            return tile

        w1_c = [keep.tile([P, BANK], U32, name=f"w1_c{b}", align_bytes=64) for b in range(2)]
        w1_s = [keep.tile([P, BANK], U8, name=f"w1_s{b}", align_bytes=64) for b in range(2)]

        def prepare_w1(b, raw, tag):
            rounded = keep.tile([P, 4 * BANK], BF16, name=f"w1_bf{b}", tag=tag, align_bytes=64)
            nc.scalar.copy(
                rounded[:].rearrange("p (t c j) -> p c t j", t=4, j=4),
                raw[:].rearrange("p j (c t) -> p c t j", t=4),
            )
            nc.vector.quantize_mx(out=w1_c[b][:].bitcast(FP8X4), scales=w1_s[b][:], in_=rounded[:])

        v_s = keep.tile([P, S], U8, name="v_s", align_bytes=64)
        v_w = [keep.tile([P, BANK], U32, name=f"v_w{half}", align_bytes=64) for half in range(2)]
        nc.vector.tensor_copy(v_s[:], tab_s[:].bitcast(U8).indirect(offs_t[:]))
        prepare_w1(0, w1_raw0, "chain_a")
        for half in range(2):
            nc.vector.tensor_copy(v_w[half][:], tab_w[:].indirect(offs_t[:, 32 * half : 32 * (half + 1)]))

        w1_raw1 = keep.tile([P, 4, BANK], F32, name="w1_raw1", tag="chain_a", align_bytes=64)
        wgt_t = keep.tile([P, M], F32, name="wgt_t", tag="chain_d", align_bytes=64)
        nc.sync.dma_start(w1_raw1[:], w1_rows[:, :, BANK:H])
        nc.sync.dma_start(wgt_t[:], wgt)
        w5_raw = placed.tile([P, 2, 4, N], F32, name="w5_raw", align_bytes=64, offset=0)
        nc.sync.dma_start(w5_raw[:], w5.rearrange("(b p j) n -> p b j n", b=2, j=4))

        work = keep.tile([P, X_RING, S], F32, name="work", align_bytes=64)
        h_of = {}
        gw_ring = [keep.tile([P, S], F32, name=f"gw{k}") for k in range(H_RING)]
        gw_of = {}
        for i, tag in enumerate(("chain_b", "chain_c")):
            gw_of[i] = keep.tile([P, S], F32, name=f"gw_first{i}", tag=tag, align_bytes=64)

        def gain_product(i, lo, hi):
            nc.vector.tensor_scalar_mul(gw_of[i][:, lo:hi], wgs_t[:, lo:hi], gain_t[:, 0, i : i + 1])

        def feature_tiles(i):
            if i == 0:
                return work[:, 0, :], gw_of[1][:]
            if i == 1:
                return work[:, 0, :], work[:, 0, :]
            gw_of[i] = gw_ring[i % H_RING]
            return gw_of[i][:], work[:, (i - 1) % X_RING, :]

        def square(i, roots, lo, hi):
            nc.scalar.activation(h_of[i][:, lo:hi], roots[:, lo:hi], ACT.Square)

        def features(i, pieces):
            b, t = divmod(i, 4)
            size, roots = feature_tiles(i)
            h_of[i] = keep.tile([P, S], F32, name=f"h{i}", tag=f"h{i % H_RING}", align_bytes=64)
            for n, (lo, hi) in enumerate(pieces):
                for c0 in range(lo, hi, BANK):
                    c1 = min(hi, c0 + BANK)
                    half, v0 = divmod(c0, BANK)
                    load = bank(2 + n if i == 0 else 6 * (i % 2) + half)
                    nc.tensor.matmul_mx(
                        out=load[:, 0 : c1 - c0],
                        lhsT=w1_c[b][:, P * t : P * (t + 1)].bitcast(FP8X4),
                        lhsT_scale=w1_s[b][:, P * t : P * (t + 1)],
                        rhs=v_w[half][:, v0 : v0 + c1 - c0].bitcast(FP8X4),
                        rhs_scale=v_s[:, c0:c1],
                        start=True,
                        stop=True,
                    )
                    nc.scalar.activation(size[:, c0:c1], load[:, 0 : c1 - c0], ACT.Abs)
                nc.scalar.activation(roots[:, lo:hi], size[:, lo:hi], ACT.Abs_reciprocal_sqrt, bias=1.0)
                if i >= 2:
                    nc.scalar.activation(size[:, lo:hi], wgs_t[:, lo:hi], ACT.Copy, scale=gain_t[:, b, t : t + 1])
                if i < LAST:
                    square(i, roots, lo, hi)
            return roots

        def scatter(i, lo, hi):
            nc.vector.tensor_tensor(
                pages[i % PAGES][:].indirect(offs2_t[:, lo // 16 : hi // 16]),
                h_of[i][:, lo:hi],
                gw_of[i][:, lo:hi],
                ALU.mult,
            )

        def gather(i, lo, hi):
            nc.vector.tensor_tensor(
                work[:, i % X_RING, lo:hi],
                pages[i % PAGES][:].indirect(offs3_t[:, lo // 16 : hi // 16]),
                wgt_t[:, lo:hi],
                ALU.mult,
            )

        z_turned = [
            [keep.tile([P, BANK], BF16, name=f"z_turned{u}_{k}", align_bytes=64) for k in range(4)] for u in range(2)
        ]
        foam_of = {}

        def add_foam(pair):
            sources = [foam_of[pair][:, e, :] for e in range(2)]
            sources = sources + [work[:, (2 * pair + e) % X_RING, :] for e in range(2)]
            sums = [bank(2 + k) for k in range(4)]
            for s in range(4):
                for k in range(4):
                    for c in range(2):
                        col = 2 * P * c + P * (s % 2)
                        m0 = 2 * P * k + P * c
                        nc.tensor.matmul(
                            sums[k][:, col : col + P],
                            sources[s][:, m0 : m0 + P],
                            ident[:],
                            start=(s, c) == (0, 0),
                            stop=(s, c) == (3, 1),
                            is_transpose=True,
                        )
            for k in range(4):
                nc.scalar.copy(
                    z_turned[pair % 2][k][:].rearrange("m (c p e) -> m c p e", c=2, e=2),
                    sums[k][:].rearrange("m (c e p) -> m c p e", c=2, e=2),
                )

        z_bf = keep.tile([P, 4 * M], BF16, name="z_bf", align_bytes=64)
        z_s0 = keep.tile([P, M], U8, name="z_s0", align_bytes=64)

        def turn_back_pass0():
            for k in range(4):
                words = bank(2 + k)
                for u in range(2):
                    for c in range(2):
                        col = 2 * P * u + P * c
                        nc.tensor.transpose(
                            words[:, col : col + P], z_turned[u][k][:].bitcast(F32)[:, P * c : P * (c + 1)], ident[:]
                        )
                nc.scalar.copy(
                    z_bf[:].bitcast(F32)[:, BANK * k : BANK * (k + 1)].rearrange("p (m u) -> p m u", u=2),
                    words[:].rearrange("p (u m) -> p m u", u=2),
                )

        z_pairs = [
            keep.tile([P, 4 * (hi - lo)], BF16, name=f"z_pairs{n}", align_bytes=64)
            for n, (lo, hi) in enumerate(LAST_PIECES)
        ]

        def turn_back_planes_4_5():
            for half in range(2):
                words = bank(half)
                for chunk in range(4):
                    k, c = divmod(4 * half + chunk, 2)
                    nc.tensor.transpose(
                        words[:, P * chunk : P * (chunk + 1)],
                        z_turned[0][k][:].bitcast(F32)[:, P * c : P * (c + 1)],
                        ident[:],
                    )
                for n, (lo, hi) in enumerate(LAST_PIECES):
                    if lo // BANK == half:
                        nc.scalar.copy(
                            z_pairs[n][:].bitcast(F32)[:, 0 : hi - lo], words[:, lo - BANK * half : hi - BANK * half]
                        )

        w5_c = keep.tile([P, 2 * N], U32, name="w5_c", align_bytes=64)
        w5_s = keep.tile([P, 2 * N], U8, name="w5_s", align_bytes=64)

        def prepare_w5():
            rounded = keep.tile([P, 2 * 4 * N], BF16, name="w5_bf", tag="chain_c", align_bytes=64)
            for b in range(2):
                nc.scalar.copy(
                    rounded[:, 4 * N * b : 4 * N * (b + 1)].rearrange("p (n j) -> p n j", j=4),
                    w5_raw[:, b].rearrange("p j n -> p n j"),
                )
            for lo, hi in ((0, BANK), (BANK, 2 * N)):
                nc.vector.quantize_mx(
                    out=w5_c[:, lo:hi].bitcast(FP8X4), scales=w5_s[:, lo:hi], in_=rounded[:, 4 * lo : 4 * hi]
                )

        def load_w4_scales():
            tile = keep.tile([P, 2 * N], U8, name="w4_s", tag="chain_c", align_bytes=64)
            nc.vector.memset(tile[:].bitcast(I32), 0)
            for quad in range(4):
                nc.sync.dma_start(
                    tile[32 * quad : 32 * quad + 4, :].bitcast(I32).rearrange("r (b c) -> r b c", b=2),
                    w4_scales[:, 4 * quad : 4 * quad + 4, :].bitcast(I32).rearrange("b r c -> r b c"),
                )
            return tile

        gain_product(0, 0, S)
        features(0, FIRST_PIECES)
        scatter(0, *FIRST_PIECES[0])
        gain_product(1, 0, BANK)
        scatter(0, *FIRST_PIECES[1])
        gain_product(1, BANK, S)
        scatter(0, *FIRST_PIECES[2])
        features(1, [(0, S)])

        def step(i):
            scatter(i + 1, 0, S)
            gather(i, 0, M)
            return features(i + 2, [(0, S)])

        step(0)
        prepare_w1(1, w1_raw1, "chain_b")
        foam_of[0] = load_foam(0)
        foam_of[1] = load_foam(1)
        step(1)
        prepare_w5()
        w4_s = load_w4_scales()
        step(2)
        step(3)
        add_foam(0)
        foam_of[2] = load_foam(2)
        step(4)
        last_roots = step(5)
        add_foam(1)
        foam_of[3] = load_foam(3)
        turn_back_pass0()
        square(LAST, last_roots, 0, S)
        scatter(LAST, 0, S)
        add_foam(2)
        turn_back_planes_4_5()
        z_c0 = keep.tile([P, M], U32, name="z_c0", tag=f"h{LAST % H_RING}", align_bytes=64)
        nc.vector.quantize_mx(out=z_c0[:].bitcast(FP8X4), scales=z_s0[:], in_=z_bf[:])
        w4_w = keep.tile([P, 2 * 2 * N], U8, name="w4_w", tag="z_turned1_0", align_bytes=64)
        nc.sync.dma_start(
            w4_w[:].bitcast(I32).rearrange("p (b c) -> p b c", b=2), w4_words.bitcast(I32).rearrange("b p c -> p b c")
        )

        def passes(sums, b, codes, scales):
            for nt in range(N_TILES):
                col = N * b + P * nt
                flags = dict(start=(b == 0 and nt == 0), stop=(b == 1 and nt == N_TILES - 1))
                nc.tensor.matmul_mx(
                    out=sums[0][:, P * nt : P * (nt + 1)],
                    lhsT=w4_w[:, 2 * col : 2 * (col + P)].bitcast(FP4X4),
                    lhsT_scale=w4_s[:, col : col + P],
                    rhs=codes.bitcast(FP8X4),
                    rhs_scale=scales,
                    **flags,
                )
                nc.tensor.matmul_mx(
                    out=sums[1][:, P * nt : P * (nt + 1)],
                    lhsT=w5_c[:, col : col + P].bitcast(FP8X4),
                    lhsT_scale=w5_s[:, col : col + P],
                    rhs=codes.bitcast(FP8X4),
                    rhs_scale=scales,
                    **flags,
                )

        def open_sums(chunk):
            sums = (bank(2 * chunk % BANKS), bank((2 * chunk + 1) % BANKS))
            cols = slice(P * chunk, P * (chunk + 1))
            passes(sums, 0, z_c0[:, cols], z_s0[:, cols])
            return sums

        opened = {chunk: open_sums(chunk) for chunk in range(BANKS // 2)}
        out_rows = out.rearrange("(nt p) m -> p nt m", p=P)
        quantised = {}

        def make_z(n):
            lo, hi = LAST_PIECES[n]
            width = hi - lo
            if lo % BANK == 0:
                gather(LAST - 1, lo, lo + BANK)
            gather(LAST, lo, hi)
            nc.vector.tensor_tensor(
                z_pairs[n][:, 2 * width : 4 * width].rearrange("p (c i e) -> p c e i", i=4, e=2),
                work[:, 0:2, lo:hi].rearrange("p e (c i) -> p c e i", i=4),
                foam_of[3][:, :, lo:hi].rearrange("p e (c i) -> p c e i", i=4),
                ALU.add,
            )
            nc.scalar.copy(
                z_bf[:].bitcast(F32)[:, 2 * lo : 2 * hi].rearrange("p (m u) -> p m u", u=2),
                z_pairs[n][:].bitcast(F32).rearrange("p (u m) -> p m u", u=2),
            )

        def quantise_z(n):
            lo, hi = LAST_PIECES[n]
            z_c = keep.tile([P, hi - lo], U32, name=f"z_c1_{n}", align_bytes=64)
            z_s = keep.tile([P, hi - lo], U8, name=f"z_s1_{n}", align_bytes=64)
            nc.vector.quantize_mx(out=z_c[:].bitcast(FP8X4), scales=z_s[:], in_=z_bf[:, 4 * lo : 4 * hi])
            quantised[n] = (z_c, z_s)

        def finish(n):
            lo, hi = LAST_PIECES[n]
            z_c, z_s = quantised[n]
            result = keep.tile([P, N_TILES, hi - lo], F32, name=f"result{n}")
            for c in range((hi - lo) // P):
                chunk = lo // P + c
                sums = opened[chunk] if chunk in opened else open_sums(chunk)
                cols = slice(P * c, P * (c + 1))
                passes(sums, 1, z_c[:, cols], z_s[:, cols])
                wear = ring.tile([P, N], F32, name="wear")
                nc.scalar.activation(wear[:], sums[0][:, 0:N], ACT.Abs)
                nc.vector.tensor_tensor(
                    result[:, :, cols],
                    wear[:].rearrange("p (nt m) -> p nt m", nt=N_TILES),
                    sums[1][:, 0:N].rearrange("p (nt m) -> p nt m", nt=N_TILES),
                    ALU.subtract,
                )
            nc.sync.dma_start(out_rows[:, :, lo:hi], result[:])

        count = len(LAST_PIECES)
        for n in range(count + 2):
            if n < count:
                make_z(n)
            if 1 <= n <= count:
                quantise_z(n - 1)
            if n >= 2:
                finish(n - 2)
